import numpy as np
import ml_dtypes


def mxq(x, axis, fmt="e4m3"):
    dtype, down = {"e4m3": (ml_dtypes.float8_e4m3fn, 7), "e5m2": (ml_dtypes.float8_e5m2, 14)}[fmt]
    v = np.moveaxis(np.asarray(x, np.float32).astype(ml_dtypes.bfloat16).astype(np.float64), axis, -1)
    blocks = v.reshape(v.shape[:-1] + (-1, 32))
    amax = np.abs(blocks).max(-1, keepdims=True)
    byte = np.maximum(np.where(amax > 0, np.frexp(amax)[1] - 1 + 127, 0) - down, 1)
    scale = np.exp2(byte - 127.0)
    codes = (blocks / scale).astype(np.float32).astype(dtype).astype(np.float64)
    return np.moveaxis((codes * scale).reshape(v.shape), -1, axis)


WIDE = False


def mx_kscale(k):
    if not WIDE:
        return np.ones(k)
    levels = np.array([10, -10, 5, -5, 0])
    if k % 512:
        return np.exp2(np.random.permutation(np.resize(levels, k // 32))).repeat(32)
    a = np.empty((k // 512, 16))
    for p in range(k // 512):
        a[p, :8] = np.random.permutation(np.resize(levels, 8))
        for g in range(8):
            far = levels[np.abs(levels - a[p, g]) >= 10]
            a[p, g + 8] = far[np.random.randint(len(far))]
    return np.exp2(a.ravel()).repeat(32)


def f64(x):
    return np.asarray(x).astype(np.float64)


def striped(idx):
    return np.tile(idx.reshape(-1, 16).T, (8, 1)).astype(np.uint16)


def unstriped(offs):
    return offs[:16].T.reshape(-1).astype(np.int64)


E2M1 = np.array([0.0, 0.5, 1.0, 1.5, 2.0, 3.0, 4.0, 6.0, -0.0, -0.5, -1.0, -1.5, -2.0, -3.0, -4.0, -6.0])


def pack_weight(w, fmt):
    k, n = w.shape
    w = f64(np.asarray(w, np.float32).astype(ml_dtypes.bfloat16)).reshape(k // 32, 32, n)
    amax = np.abs(w).max(1)
    if fmt == "e4m3":
        byte = np.frexp(amax)[1] - 1 + 127 - 7
    else:
        mant, ex = np.frexp(amax / 6.0)
        byte = np.where(mant > 0.5, ex, ex - 1) + 127
    byte = np.clip(np.where(amax > 0, byte, 1), 1, 254)
    scaled = (w * np.exp2(127.0 - byte)[:, None, :]).reshape(k, n).astype(np.float32)
    by_word = np.ascontiguousarray(scaled.reshape(k // 512, 128, 4, n).transpose(0, 1, 3, 2))
    if fmt == "e4m3":
        words = by_word.astype(ml_dtypes.float8_e4m3fn).view(np.uint8)
    else:
        c = by_word.astype(ml_dtypes.float4_e2m1fn).view(np.uint8) & 0xF
        words = (c[..., 0::2] | (c[..., 1::2] << 4)).reshape(k // 512, 128, 2 * n)
    return np.ascontiguousarray(words), np.ascontiguousarray(byte.astype(np.uint8).reshape(k // 512, 16, n))


def unpack_weight(words, scales, fmt):
    g, _, n = scales.shape
    words = np.ascontiguousarray(words).reshape(g, 128, n, -1)
    if fmt == "e4m3":
        vals = words.view(ml_dtypes.float8_e4m3fn).astype(np.float64)
    else:
        nib = np.empty((g, 128, n, 4), np.uint8)
        nib[..., 0::2] = words & 0xF
        nib[..., 1::2] = words >> 4
        vals = E2M1[nib]
    vals = vals * np.repeat(np.exp2(scales.astype(np.float64) - 127.0), 8, axis=1)[..., None]
    return vals.transpose(0, 1, 3, 2).reshape(g * 512, n)


def gelu(v):
    return 0.5 * v * (1.0 + np.tanh(np.sqrt(2.0 / np.pi) * (v + 0.044715 * v**3)))


K, T, E, C, H, TOP, COPIES = 512, 768, 6, 256, 512, 3, 384
PAD = 64


def by_expert(wq, xq):
    return np.concatenate([wq[e].T @ xq[:, e * C:(e + 1) * C] for e in range(E)], axis=1)


def setup_inputs():
    n = np.random.standard_normal
    s = mx_kscale(K)
    u = mx_kscale(H)
    left = TOP * T - E * C - COPIES
    deal = np.repeat(np.arange(E + 2), [C] * E + [COPIES, left]).reshape(TOP, T)[:, np.random.permutation(T)]
    deal = np.take_along_axis(deal, np.argsort(np.random.rand(TOP, T), axis=0), axis=0)
    for _ in range(8):
        s_, t_ = np.random.permutation(T).reshape(2, -1); r = np.random.randint(TOP, size=T // 2); x, y = deal[r, s_].copy(), deal[r, t_].copy()
        ok = ~((deal[:, s_] == y).any(0) | (deal[:, t_] == x).any(0)); deal[r[ok], s_[ok]] = y[ok]; deal[r[ok], t_[ok]] = x[ok]
    order = np.lexsort((np.random.rand(TOP * T), deal.reshape(-1)))[:E * C]
    slot_token = order % T
    pos = np.where(deal == E, E * C + np.arange(T), E * C + T + np.arange(T) % PAD).reshape(-1); pos[order] = np.arange(E * C); pos = pos.reshape(TOP, T)
    g = np.random.uniform(0.5, 1.5, (TOP, T)); g = g / g.sum(0)
    xf = n((K, T))
    x = pack_weight(xf * s[:, None], "e4m3")
    w1 = [pack_weight(m, "e4m3") for m in n((E, K, H)) / np.sqrt(K) / s[None, :, None]]
    w3 = [pack_weight(m, "e4m3") for m in n((E, K, H)) / np.sqrt(K) / s[None, :, None] * u]
    w2 = [pack_weight(m, "e4m3") for m in n((E, H, K)) / np.sqrt(H) / u[None, :, None]]
    return {
        "x_words": x[0],
        "x_scales": x[1],
        "xr": (xf).astype(np.float32),
        "w1_words": np.stack([m[0] for m in w1]),
        "w1_scales": np.stack([m[1] for m in w1]),
        "w3_words": np.stack([m[0] for m in w3]),
        "w3_scales": np.stack([m[1] for m in w3]),
        "w2_words": np.stack([m[0] for m in w2]),
        "w2_scales": np.stack([m[1] for m in w2]),
        "gate": np.stack([np.tile(r, (128, 1)) for r in g]).astype(np.float32),
        "offs": striped(slot_token),
        "pos1": striped(pos[0]),
        "pos2": striped(pos[1]),
        "pos3": striped(pos[2]),
    }


def reference(x_words, x_scales, xr, w1_words, w1_scales, w3_words, w3_scales, w2_words, w2_scales, gate, offs, pos1, pos2, pos3):
    w1 = np.stack([unpack_weight(w1_words[e], w1_scales[e], "e4m3") for e in range(E)])
    w3 = np.stack([unpack_weight(w3_words[e], w3_scales[e], "e4m3") for e in range(E)])
    w2 = np.stack([unpack_weight(w2_words[e], w2_scales[e], "e4m3") for e in range(E)])
    idx = unstriped(offs)
    xq = unpack_weight(x_words, x_scales, "e4m3")[:, idx]
    h = gelu(by_expert(w1, xq)) * by_expert(w3, xq)
    y = by_expert(w2, mxq(h, 0, "e4m3"))
    y = np.concatenate([y, f64(xr), np.zeros((K, PAD))], axis=1)
    out = sum(f64(gate[r, :1]) * y[:, unstriped(p)] for r, p in enumerate((pos1, pos2, pos3)))
    return out

@@ -1,0 +1,214 @@
+from contextlib import ExitStack
+
+import concourse.mybir as mybir
+from concourse.masks import make_identity
+
+K, T, E, C, H, TOP, PAD = 512, 768, 6, 256, 512, 3, 64
+S = E * C
+W = S + T + PAD
+FLOPS = 2 * S * (2 * K * H + H * K)
+
+F32 = mybir.dt.float32
+BF16 = mybir.dt.bfloat16
+I32 = mybir.dt.int32
+U32 = mybir.dt.uint32
+U16 = mybir.dt.uint16
+U8 = mybir.dt.uint8
+FP8X4 = mybir.dt.float8_e4m3fn_x4
+MULT = mybir.AluOpType.mult
+ADD = mybir.AluOpType.add
+GELU = mybir.ActivationFunctionType.Gelu_apprx_tanh
+
+P = 128
+W1_ROW, W3_ROW, W2_ROW = 4, 8, 12
+NB = K // P
+
+
+def tile_moe_cpy_glu_gelu_kernel(
+    tc, x_words, x_scales, xr, w1_words, w1_scales, w3_words, w3_scales, w2_words, w2_scales, gate, offs, pos1, pos2, pos3, out
+):
+    nc = tc.nc
+    with ExitStack() as ctx:
+        keep = ctx.enter_context(tc.tile_pool(name="keep", bufs=1))
+        ring = ctx.enter_context(tc.tile_pool(name="ring", bufs=3))
+        pair = ctx.enter_context(tc.tile_pool(name="pair", bufs=2))
+        psum = ctx.enter_context(tc.psum_pool(name="psum", bufs=2))
+
+        offs_t = keep.tile([P, S // 16], U16, name="offs_t")
+        pos_t = [keep.tile([P, T // 16], U16, name="pos%d_t" % r) for r in range(TOP)]
+        xw = keep.tile([P, T], I32, name="xw", align_bytes=64)
+        xs = keep.tile([P, T // 4], I32, name="xs", align_bytes=64)
+        xgw = keep.tile([P, S], U32, name="xgw", align_bytes=64)
+        xgs = keep.tile([P, S], U8, name="xgs", align_bytes=64)
+        w1 = [keep.tile([P, H], I32, name="w1_%d" % e, align_bytes=64) for e in range(E)]
+        w3 = [keep.tile([P, H], I32, name="w3_%d" % e, align_bytes=64) for e in range(E)]
+        w2 = [keep.tile([P, K], I32, name="w2_%d" % e, align_bytes=64) for e in range(E)]
+        w1s = keep.tile([P, E * H // 4], I32, name="w1s", align_bytes=64)
+        w3s = keep.tile([P, E * H // 4], I32, name="w3s", align_bytes=64)
+        w2s = keep.tile([P, E * K // 4], I32, name="w2s", align_bytes=64)
+        hq = keep.tile([P, S], U32, name="hq", align_bytes=64)
+        hs = keep.tile([P, S], U8, name="hs", align_bytes=64)
+        y = [keep.tile([P, W], F32, name="y%d" % b, align_bytes=64) for b in range(NB)]
+        g_t = [keep.tile([P, T], F32, name="gate%d" % r, align_bytes=64) for r in range(TOP)]
+        ident = keep.tile([P, P], F32, name="ident", align_bytes=64)
+        zeros = keep.tile([P, PAD], F32, name="zeros")
+
+        def load_scales(tile, row, src):
+            for q in range(4):
+                nc.sync.dma_start(
+                    out=tile[32 * q + row : 32 * q + row + 4, :].rearrange("r (e n) -> r e n", e=src.shape[0]),
+                    in_=src[:, 4 * q : 4 * q + 4, :].bitcast(I32).rearrange("e r n -> r e n"),
+                )
+
+        def load_words(tile, src):
+            nc.sync.dma_start(out=tile[:], in_=src.rearrange("p n d -> p (n d)").bitcast(I32))
+
+        for plane in (xs, w1s, w3s, w2s):
+            nc.vector.memset(plane[:], 0)
+        nc.gpsimd.memset(zeros[:], 0.0)
+        make_identity(nc, ident[:])
+        for b in range(NB):
+            nc.scalar.activation(y[b][:, S + T : W], zeros[:], GELU)
+
+        nc.sync.dma_start(offs_t[:], offs)
+        load_words(xw, x_words[0])
+        load_scales(xs, 0, x_scales)
+        load_words(w1[0], w1_words[0, 0])
+        load_scales(w1s, W1_ROW, w1_scales[:, 0])
+        load_scales(w3s, W3_ROW, w3_scales[:, 0])
+        load_words(w3[0], w3_words[0, 0])
+        load_words(w1[1], w1_words[1, 0])
+        load_words(w3[1], w3_words[1, 0])
+        load_scales(w2s, W2_ROW, w2_scales[:, 0])
+        for e in range(E):
+            if e + 2 < E:
+                load_words(w1[e + 2], w1_words[e + 2, 0])
+                load_words(w3[e + 2], w3_words[e + 2, 0])
+            load_words(w2[e], w2_words[e, 0])
+        for r, pos in enumerate((pos1, pos2, pos3)):
+            nc.sync.dma_start(pos_t[r][:], pos)
+        nc.sync.dma_start(out=y[0][:, S : S + T], in_=xr[0:P, :])
+        for r in range(TOP):
+            nc.sync.dma_start(out=g_t[r][:], in_=gate[r])
+        for b in range(1, NB):
+            nc.sync.dma_start(out=y[b][:, S : S + T], in_=xr[b * P : (b + 1) * P, :])
+
+        def gather_tokens(e):
+            cols = slice(e * C, (e + 1) * C)
+            lst = offs_t[:, e * C // 16 : (e + 1) * C // 16]
+            nc.vector.tensor_copy(xgw[:, cols], xw[:].bitcast(U32).indirect(lst))
+            nc.vector.tensor_copy(xgs[:, cols], xs[:].bitcast(U8).indirect(lst))
+
+        def first_layer(j):
+            e = j // 2
+            cols = slice(j * P, (j + 1) * P)
+            scols = slice(e * H // 4, (e + 1) * H // 4)
+            a = psum.tile([P, H], F32, name="a", tag="a")
+            b = psum.tile([P, H], F32, name="b", tag="b")
+            for acc, wt, ws, row in ((a, w1[e], w1s, W1_ROW), (b, w3[e], w3s, W3_ROW)):
+                nc.tensor.matmul_mx(
+                    out=acc[:], lhsT=xgw[:, cols].bitcast(FP8X4), lhsT_scale=xgs[:, cols],
+                    rhs=wt[:].bitcast(FP8X4), rhs_scale=ws[row:P, scols].bitcast(U8), start=True, stop=True,
+                )
+            act = ring.tile([P, H], F32, name="act", align_bytes=64)
+            nc.scalar.activation(
+                act[:].rearrange("s (u p v) -> s u p v", u=2, v=2), a[:].rearrange("s (p u v) -> s u p v", u=2, v=2), GELU
+            )
+            h = ring.tile([P, H], BF16, name="h", align_bytes=64)
+            nc.vector.tensor_tensor(
+                h[:].rearrange("s (u p v) -> s u p v", u=2, v=2),
+                act[:].rearrange("s (u p v) -> s u p v", u=2, v=2),
+                b[:].rearrange("s (p u v) -> s u p v", u=2, v=2),
+                MULT,
+            )
+            return h
+
+        def quantise(j0, tiles):
+            n = len(tiles)
+            tb = psum.tile([P, n, 2, P], F32, name="tb", tag="t")
+            for i, h in enumerate(tiles):
+                for u in range(2):
+                    nc.tensor.transpose(tb[:, i, u, :], h[:, u * 256 : (u + 1) * 256].bitcast(F32), ident[:])
+            ht = pair.tile([P, n * P * 4], BF16, name="ht", align_bytes=64)
+            nc.scalar.copy(ht[:].bitcast(F32).rearrange("p (i s u) -> p i s u", i=n, u=2), tb[:].rearrange("p i u s -> p i s u"))
+            cols = slice(j0 * P, (j0 + n) * P)
+            nc.vector.quantize_mx(out=hq[:, cols].bitcast(FP8X4), scales=hs[:, cols], in_=ht[:])
+
+        def second_layer(b, c0, widths):
+            total = sum(widths)
+            yb = psum.tile([P, total], F32, name="yb", tag="y")
+            c = c0
+            for wd in widths:
+                e = c // C
+                sc = e * K // 4 + b * P // 4
+                nc.tensor.matmul_mx(
+                    out=yb[:, c - c0 : c - c0 + wd], lhsT=w2[e][:, b * P : (b + 1) * P].bitcast(FP8X4),
+                    lhsT_scale=w2s[W2_ROW:P, sc : sc + P // 4].bitcast(U8),
+                    rhs=hq[:, c : c + wd].bitcast(FP8X4), rhs_scale=hs[:, c : c + wd], start=True, stop=True,
+                )
+                c += wd
+            nc.scalar.copy(y[b][:, c0 : c0 + total], yb[:])
+
+        gather_tokens(0)
+        gather_tokens(1)
+        for e in range(E):
+            h0 = first_layer(2 * e)
+            h1 = first_layer(2 * e + 1)
+            if e + 2 < E:
+                gather_tokens(e + 2)
+            if e < E - 1:
+                quantise(2 * e, [h0, h1])
+            else:
+                quantise(2 * e, [h0])
+                second_layer(0, 2 * e * P, [P])
+                quantise(2 * e + 1, [h1])
+                second_layer(0, (2 * e + 1) * P, [P])
+            if e in (1, 3):
+                second_layer(0, (e - 1) * C, [C, C])
+            if e == 4:
+                second_layer(0, e * C, [C])
+
+        def products(b, t0, t1):
+            prods = []
+            for r in range(TOP):
+                pr = pair.tile([P, t1 - t0], F32, name="prod%d" % r, align_bytes=64)
+                nc.vector.tensor_tensor(pr[:], y[b][:].indirect(pos_t[r][:, t0 // 16 : t1 // 16]), g_t[r][:, t0:t1], MULT)
+                prods.append(pr)
+            return prods
+
+        def sum_on_tensor(b, prods, p0, t0, n):
+            sb = psum.tile([P, n, P], F32, name="sb", tag="a")
+            for i in range(n):
+                c = t0 - p0 + i * P
+                for r in range(TOP):
+                    nc.tensor.matmul(
+                        sb[:, i, :], lhsT=prods[r][:, c : c + P], rhs=ident[:], start=(r == 0), stop=(r == TOP - 1), is_transpose=True
+                    )
+            st = pair.tile([P, n, P], F32, name="st", align_bytes=64)
+            nc.scalar.copy(st[:], sb[:])
+            bb = psum.tile([P, n, P], F32, name="bb", tag="b")
+            for i in range(n):
+                nc.tensor.transpose(bb[:, i, :], st[:, i, :], ident[:])
+            o = ring.tile([P, n * P], F32, name="o", align_bytes=64)
+            nc.scalar.copy(o[:], bb[:].rearrange("p i t -> p (i t)"))
+            nc.sync.dma_start(out=out[b * P : (b + 1) * P, t0 : t0 + n * P], in_=o[:])
+
+        half = T // 2
+        prods = products(0, 0, T)
+        for b in range(1, NB):
+            for e in range(0, E, 2):
+                second_layer(b, e * C, [C, C])
+        for b in range(NB - 1):
+            sum_on_tensor(b, prods, 0, 0, 3)
+            sum_on_tensor(b, prods, 0, half, 3)
+            if b + 1 < NB - 1:
+                prods = products(b + 1, 0, T)
+        b = NB - 1
+        prods = products(b, 0, half)
+        sum_on_tensor(b, prods, 0, 0, 3)
+        prods = products(b, half, T)
+        s12 = pair.tile([P, half], F32, name="s12", align_bytes=64)
+        nc.vector.tensor_tensor(s12[:], prods[0][:], prods[1][:], ADD)
+        o = ring.tile([P, half], F32, name="o", align_bytes=64)
+        nc.vector.tensor_tensor(o[:], s12[:], prods[2][:], ADD)
+        nc.sync.dma_start(out=out[b * P : (b + 1) * P, half:T], in_=o[:])

@@ -30,91 +30,94 @@ def tile_moe_cpy_glu_gelu_kernel(
     nc = tc.nc
     with ExitStack() as ctx:
         keep = ctx.enter_context(tc.tile_pool(name="keep", bufs=1))
-        ring = ctx.enter_context(tc.tile_pool(name="ring", bufs=3))
+        ring = ctx.enter_context(tc.tile_pool(name="ring", bufs=4))
         pair = ctx.enter_context(tc.tile_pool(name="pair", bufs=2))
+        trio = ctx.enter_context(tc.tile_pool(name="trio", bufs=4))
         psum = ctx.enter_context(tc.psum_pool(name="psum", bufs=2))
 
         offs_t = keep.tile([P, S // 16], U16, name="offs_t")
         pos_t = [keep.tile([P, T // 16], U16, name="pos%d_t" % r) for r in range(TOP)]
         xw = keep.tile([P, T], I32, name="xw", align_bytes=64)
         xs = keep.tile([P, T // 4], I32, name="xs", align_bytes=64)
-        xgw = keep.tile([P, S], U32, name="xgw", align_bytes=64)
-        xgs = keep.tile([P, S], U8, name="xgs", align_bytes=64)
-        w1 = [keep.tile([P, H], I32, name="w1_%d" % e, align_bytes=64) for e in range(E)]
-        w3 = [keep.tile([P, H], I32, name="w3_%d" % e, align_bytes=64) for e in range(E)]
-        w2 = [keep.tile([P, K], I32, name="w2_%d" % e, align_bytes=64) for e in range(E)]
-        w1s = keep.tile([P, E * H // 4], I32, name="w1s", align_bytes=64)
-        w3s = keep.tile([P, E * H // 4], I32, name="w3s", align_bytes=64)
+        w1 = keep.tile([P, E, H], I32, name="w1", align_bytes=64)
+        w3 = keep.tile([P, E, H], I32, name="w3", align_bytes=64)
+        w2 = keep.tile([P, E, K], I32, name="w2", align_bytes=64)
+        w13s = keep.tile([P, E * H // 4], I32, name="w13s", align_bytes=64)
         w2s = keep.tile([P, E * K // 4], I32, name="w2s", align_bytes=64)
         hq = keep.tile([P, S], U32, name="hq", align_bytes=64)
         hs = keep.tile([P, S], U8, name="hs", align_bytes=64)
         y = [keep.tile([P, W], F32, name="y%d" % b, align_bytes=64) for b in range(NB)]
-        g_t = [keep.tile([P, T], F32, name="gate%d" % r, align_bytes=64) for r in range(TOP)]
+        g_t = keep.tile([P, TOP, T], F32, name="g_t", align_bytes=64)
         ident = keep.tile([P, P], F32, name="ident", align_bytes=64)
         zeros = keep.tile([P, PAD], F32, name="zeros")
 
-        def load_scales(tile, row, src):
+        def load_scales(eng, tile, row, src):
             for q in range(4):
-                nc.sync.dma_start(
+                eng.dma_start(
                     out=tile[32 * q + row : 32 * q + row + 4, :].rearrange("r (e n) -> r e n", e=src.shape[0]),
                     in_=src[:, 4 * q : 4 * q + 4, :].bitcast(I32).rearrange("e r n -> r e n"),
                 )
 
-        def load_words(tile, src):
-            nc.sync.dma_start(out=tile[:], in_=src.rearrange("p n d -> p (n d)").bitcast(I32))
+        def load_words(tile, src, e0, e1):
+            nc.sync.dma_start(out=tile[:, e0:e1, :], in_=src[e0:e1, 0].rearrange("e p n d -> p e (n d)").bitcast(I32))
 
-        for plane in (xs, w1s, w3s, w2s):
-            nc.vector.memset(plane[:], 0)
-        nc.gpsimd.memset(zeros[:], 0.0)
+        nc.vector.memset(w13s[:, : E * H // 8], 0)
+        nc.gpsimd.memset(w13s[:, E * H // 8 :], 0)
+        nc.vector.memset(zeros[:], 0.0)
+        nc.vector.memset(w2s[:], 0)
         make_identity(nc, ident[:])
-        for b in range(NB):
-            nc.scalar.activation(y[b][:, S + T : W], zeros[:], GELU)
 
         nc.sync.dma_start(offs_t[:], offs)
-        load_words(xw, x_words[0])
-        load_scales(xs, 0, x_scales)
-        load_words(w1[0], w1_words[0, 0])
-        load_scales(w1s, W1_ROW, w1_scales[:, 0])
-        load_scales(w3s, W3_ROW, w3_scales[:, 0])
-        load_words(w3[0], w3_words[0, 0])
-        load_words(w1[1], w1_words[1, 0])
-        load_words(w3[1], w3_words[1, 0])
-        load_scales(w2s, W2_ROW, w2_scales[:, 0])
-        for e in range(E):
-            if e + 2 < E:
-                load_words(w1[e + 2], w1_words[e + 2, 0])
-                load_words(w3[e + 2], w3_words[e + 2, 0])
-            load_words(w2[e], w2_words[e, 0])
+        for q, eng in enumerate((nc.scalar, nc.scalar, nc.sync, nc.sync)):
+            eng.dma_start(
+                out=xs[32 * q : 32 * q + 32, :],
+                in_=x_scales[:, 4 * q : 4 * q + 4, :].bitcast(I32).broadcast_to([8, 4, T // 4]),
+            )
+        nc.sync.dma_start(out=xw[:], in_=x_words[0].rearrange("p t d -> p (t d)").bitcast(I32))
+        load_scales(nc.sync, w13s, W1_ROW, w1_scales[:, 0])
+        load_scales(nc.scalar, w13s, W3_ROW, w3_scales[:, 0])
+        for e0, e1 in ((0, 1), (1, 3)):
+            load_words(w1, w1_words, e0, e1)
+            load_words(w3, w3_words, e0, e1)
+        load_scales(nc.sync, w2s, W2_ROW, w2_scales[:, 0])
+        load_words(w1, w1_words, 3, E)
+        load_words(w3, w3_words, 3, E)
+        load_words(w2, w2_words, 0, 3)
+        load_words(w2, w2_words, 3, E)
+        nc.sync.dma_start(out=y[0][:, S : S + T], in_=xr[0:P, :])
+        nc.sync.dma_start(out=g_t[:], in_=gate.rearrange("r p t -> p r t"))
         for r, pos in enumerate((pos1, pos2, pos3)):
             nc.sync.dma_start(pos_t[r][:], pos)
-        nc.sync.dma_start(out=y[0][:, S : S + T], in_=xr[0:P, :])
-        for r in range(TOP):
-            nc.sync.dma_start(out=g_t[r][:], in_=gate[r])
         for b in range(1, NB):
             nc.sync.dma_start(out=y[b][:, S : S + T], in_=xr[b * P : (b + 1) * P, :])
 
-        def gather_tokens(e):
-            cols = slice(e * C, (e + 1) * C)
-            lst = offs_t[:, e * C // 16 : (e + 1) * C // 16]
-            nc.vector.tensor_copy(xgw[:, cols], xw[:].bitcast(U32).indirect(lst))
-            nc.vector.tensor_copy(xgs[:, cols], xs[:].bitcast(U8).indirect(lst))
+        for b in range(NB):
+            nc.scalar.activation(y[b][:, S + T : W], zeros[:], GELU)
 
-        def first_layer(j):
+        def gather_tokens(e):
+            lst = offs_t[:, e * C // 16 : (e + 1) * C // 16]
+            xgw = trio.tile([P, C], U32, name="xgw", align_bytes=64)
+            xgs = trio.tile([P, C], U8, name="xgs", align_bytes=64)
+            nc.vector.tensor_copy(xgw[:], xw[:].bitcast(U32).indirect(lst))
+            nc.vector.tensor_copy(xgs[:], xs[:].bitcast(U8).indirect(lst))
+            return xgw, xgs
+
+        def first_layer(j, xgw, xgs):
             e = j // 2
-            cols = slice(j * P, (j + 1) * P)
+            cols = slice(j % 2 * P, (j % 2 + 1) * P)
             scols = slice(e * H // 4, (e + 1) * H // 4)
-            a = psum.tile([P, H], F32, name="a", tag="a")
-            b = psum.tile([P, H], F32, name="b", tag="b")
-            for acc, wt, ws, row in ((a, w1[e], w1s, W1_ROW), (b, w3[e], w3s, W3_ROW)):
+            a = psum.tile([P, H], F32, name="a", tag="a", bufs=2)
+            b = psum.tile([P, H], F32, name="b", tag="b", bufs=3)
+            for acc, wt, ws, row in ((a, w1, w13s, W1_ROW), (b, w3, w13s, W3_ROW)):
                 nc.tensor.matmul_mx(
                     out=acc[:], lhsT=xgw[:, cols].bitcast(FP8X4), lhsT_scale=xgs[:, cols],
-                    rhs=wt[:].bitcast(FP8X4), rhs_scale=ws[row:P, scols].bitcast(U8), start=True, stop=True,
+                    rhs=wt[:, e, :].bitcast(FP8X4), rhs_scale=ws[row:P, scols].bitcast(U8), start=True, stop=True,
                 )
-            act = ring.tile([P, H], F32, name="act", align_bytes=64)
+            act = ring.tile([P, H], F32, name="act", align_bytes=64, bufs=6)
             nc.scalar.activation(
                 act[:].rearrange("s (u p v) -> s u p v", u=2, v=2), a[:].rearrange("s (p u v) -> s u p v", u=2, v=2), GELU
             )
-            h = ring.tile([P, H], BF16, name="h", align_bytes=64)
+            h = ring.tile([P, H], BF16, name="h", align_bytes=64, bufs=12)
             nc.vector.tensor_tensor(
                 h[:].rearrange("s (u p v) -> s u p v", u=2, v=2),
                 act[:].rearrange("s (u p v) -> s u p v", u=2, v=2),
@@ -125,59 +128,59 @@ def tile_moe_cpy_glu_gelu_kernel(
 
         def quantise(j0, tiles):
             n = len(tiles)
-            tb = psum.tile([P, n, 2, P], F32, name="tb", tag="t")
+            tb = psum.tile([P, n, 2, P], F32, name="tb", tag="t", bufs=3)
             for i, h in enumerate(tiles):
                 for u in range(2):
                     nc.tensor.transpose(tb[:, i, u, :], h[:, u * 256 : (u + 1) * 256].bitcast(F32), ident[:])
-            ht = pair.tile([P, n * P * 4], BF16, name="ht", align_bytes=64)
+            ht = pair.tile([P, n * P * 4], BF16, name="ht", align_bytes=64, bufs=7)
             nc.scalar.copy(ht[:].bitcast(F32).rearrange("p (i s u) -> p i s u", i=n, u=2), tb[:].rearrange("p i u s -> p i s u"))
             cols = slice(j0 * P, (j0 + n) * P)
             nc.vector.quantize_mx(out=hq[:, cols].bitcast(FP8X4), scales=hs[:, cols], in_=ht[:])
 
-        def second_layer(b, c0, widths):
+        def second_layer(b, c0, widths, tag, bufs, on_vector=False):
             total = sum(widths)
-            yb = psum.tile([P, total], F32, name="yb", tag="y")
+            yb = psum.tile([P, total], F32, name="yb", tag=tag, bufs=bufs)
             c = c0
             for wd in widths:
                 e = c // C
                 sc = e * K // 4 + b * P // 4
                 nc.tensor.matmul_mx(
-                    out=yb[:, c - c0 : c - c0 + wd], lhsT=w2[e][:, b * P : (b + 1) * P].bitcast(FP8X4),
+                    out=yb[:, c - c0 : c - c0 + wd], lhsT=w2[:, e, b * P : (b + 1) * P].bitcast(FP8X4),
                     lhsT_scale=w2s[W2_ROW:P, sc : sc + P // 4].bitcast(U8),
                     rhs=hq[:, c : c + wd].bitcast(FP8X4), rhs_scale=hs[:, c : c + wd], start=True, stop=True,
                 )
                 c += wd
-            nc.scalar.copy(y[b][:, c0 : c0 + total], yb[:])
-
-        gather_tokens(0)
-        gather_tokens(1)
-        for e in range(E):
-            h0 = first_layer(2 * e)
-            h1 = first_layer(2 * e + 1)
-            if e + 2 < E:
-                gather_tokens(e + 2)
-            if e < E - 1:
-                quantise(2 * e, [h0, h1])
+            if on_vector:
+                nc.vector.tensor_copy(y[b][:, c0 : c0 + total], yb[:])
             else:
-                quantise(2 * e, [h0])
-                second_layer(0, 2 * e * P, [P])
-                quantise(2 * e + 1, [h1])
-                second_layer(0, (2 * e + 1) * P, [P])
-            if e in (1, 3):
-                second_layer(0, (e - 1) * C, [C, C])
-            if e == 4:
-                second_layer(0, e * C, [C])
+                nc.scalar.copy(y[b][:, c0 : c0 + total], yb[:])
+
+        tokens = [gather_tokens(e) for e in range(4)]
+        hidden = []
+        for j in range(2 * E):
+            hidden.append(first_layer(j, *tokens[j // 2]))
+            if j % 2 == 1 and j >= 3 and len(tokens) < E:
+                tokens.append(gather_tokens(len(tokens)))
+            if j % 2 == 1 and j >= 5:
+                quantise(j - 5, hidden[j - 5 : j - 3])
+        quantise(8, hidden[8:10])
+        quantise(10, hidden[10:11])
+        quantise(11, hidden[11:12])
+        second_layer(0, 0, [C, C], "a", 2)
+        second_layer(0, 2 * C, [C, C], "b", 3)
+        second_layer(0, 4 * C, [C, P], "a", 2, True)
+        second_layer(0, S - P, [P], "b", 3)
+
+        def product(b, r, t0, t1):
+            pr = pair.tile([P, t1 - t0], F32, name="prod%d" % r, align_bytes=64, bufs=3)
+            nc.vector.tensor_tensor(pr[:], y[b][:].indirect(pos_t[r][:, t0 // 16 : t1 // 16]), g_t[:, r, t0:t1], MULT)
+            return pr
 
         def products(b, t0, t1):
-            prods = []
-            for r in range(TOP):
-                pr = pair.tile([P, t1 - t0], F32, name="prod%d" % r, align_bytes=64)
-                nc.vector.tensor_tensor(pr[:], y[b][:].indirect(pos_t[r][:, t0 // 16 : t1 // 16]), g_t[r][:, t0:t1], MULT)
-                prods.append(pr)
-            return prods
+            return [product(b, r, t0, t1) for r in range(TOP)]
 
         def sum_on_tensor(b, prods, p0, t0, n):
-            sb = psum.tile([P, n, P], F32, name="sb", tag="a")
+            sb = psum.tile([P, n, P], F32, name="sb", tag="a", bufs=2)
             for i in range(n):
                 c = t0 - p0 + i * P
                 for r in range(TOP):
@@ -186,7 +189,7 @@ def tile_moe_cpy_glu_gelu_kernel(
                     )
             st = pair.tile([P, n, P], F32, name="st", align_bytes=64)
             nc.scalar.copy(st[:], sb[:])
-            bb = psum.tile([P, n, P], F32, name="bb", tag="b")
+            bb = psum.tile([P, n, P], F32, name="bb", tag="b", bufs=3)
             for i in range(n):
                 nc.tensor.transpose(bb[:, i, :], st[:, i, :], ident[:])
             o = ring.tile([P, n * P], F32, name="o", align_bytes=64)
@@ -197,18 +200,38 @@ def tile_moe_cpy_glu_gelu_kernel(
         prods = products(0, 0, T)
         for b in range(1, NB):
             for e in range(0, E, 2):
-                second_layer(b, e * C, [C, C])
+                second_layer(b, e * C, [C, C], "t", 3)
         for b in range(NB - 1):
             sum_on_tensor(b, prods, 0, 0, 3)
             sum_on_tensor(b, prods, 0, half, 3)
             if b + 1 < NB - 1:
                 prods = products(b + 1, 0, T)
         b = NB - 1
+        rows = slice(b * P, (b + 1) * P)
         prods = products(b, 0, half)
-        sum_on_tensor(b, prods, 0, 0, 3)
-        prods = products(b, half, T)
-        s12 = pair.tile([P, half], F32, name="s12", align_bytes=64)
-        nc.vector.tensor_tensor(s12[:], prods[0][:], prods[1][:], ADD)
+        banks = [psum.tile([P, P], F32, name="sb", tag="t", bufs=3) for i in range(3)]
+        for r in range(TOP):
+            for i in range(3):
+                nc.tensor.matmul(
+                    banks[i][:], lhsT=prods[r][:, i * P : (i + 1) * P], rhs=ident[:], start=(r == 0), stop=(r == TOP - 1), is_transpose=True
+                )
+        st = pair.tile([P, 3, P], F32, name="st", align_bytes=64)
+        bb = psum.tile([P, 3, P], F32, name="bb", tag="b", bufs=3)
+        for i in range(3):
+            nc.scalar.copy(st[:, i, :], banks[i][:])
+            nc.tensor.transpose(bb[:, i, :], st[:, i, :], ident[:])
         o = ring.tile([P, half], F32, name="o", align_bytes=64)
-        nc.vector.tensor_tensor(o[:], s12[:], prods[2][:], ADD)
-        nc.sync.dma_start(out=out[b * P : (b + 1) * P, half:T], in_=o[:])
+        nc.scalar.copy(o[:], bb[:].rearrange("p i t -> p (i t)"))
+        nc.sync.dma_start(out=out[rows, 0:half], in_=o[:])
+
+        cut = T - P
+        p1 = product(b, 0, half, T)
+        p2 = product(b, 1, half, T)
+        p3a = product(b, 2, half, cut)
+        s12 = pair.tile([P, half], F32, name="s12", align_bytes=64)
+        nc.vector.tensor_tensor(s12[:], p1[:], p2[:], ADD)
+        p3b = product(b, 2, cut, T)
+        for p3, t0, t1 in ((p3a, half, cut), (p3b, cut, T)):
+            o = ring.tile([P, t1 - t0], F32, name="o", align_bytes=64)
+            nc.vector.tensor_tensor(o[:], s12[:, t0 - half : t1 - half], p3[:], ADD)
+            nc.sync.dma_start(out=out[rows, t0:t1], in_=o[:])

@@ -22,6 +22,7 @@ GELU = mybir.ActivationFunctionType.Gelu_apprx_tanh
 P = 128
 W1_ROW, W3_ROW, W2_ROW = 4, 8, 12
 NB = K // P
+GATHER_LEAD, MULT_LAG, TURN_LAG, QUANT_LAG = 3, 1, 4, 10
 
 
 def tile_moe_cpy_glu_gelu_kernel(
@@ -32,7 +33,7 @@ def tile_moe_cpy_glu_gelu_kernel(
         keep = ctx.enter_context(tc.tile_pool(name="keep", bufs=1))
         ring = ctx.enter_context(tc.tile_pool(name="ring", bufs=4))
         pair = ctx.enter_context(tc.tile_pool(name="pair", bufs=2))
-        trio = ctx.enter_context(tc.tile_pool(name="trio", bufs=4))
+        trio = ctx.enter_context(tc.tile_pool(name="trio", bufs=3))
         psum = ctx.enter_context(tc.psum_pool(name="psum", bufs=2))
 
         offs_t = keep.tile([P, S // 16], U16, name="offs_t")
@@ -42,7 +43,8 @@ def tile_moe_cpy_glu_gelu_kernel(
         w1 = keep.tile([P, E, H], I32, name="w1", align_bytes=64)
         w3 = keep.tile([P, E, H], I32, name="w3", align_bytes=64)
         w2 = keep.tile([P, E, K], I32, name="w2", align_bytes=64)
-        w13s = keep.tile([P, E * H // 4], I32, name="w13s", align_bytes=64)
+        w1s = keep.tile([P, E * H // 4], I32, name="w1s", align_bytes=64)
+        w3s = keep.tile([P, E * H // 4], I32, name="w3s", align_bytes=64)
         w2s = keep.tile([P, E * K // 4], I32, name="w2s", align_bytes=64)
         hq = keep.tile([P, S], U32, name="hq", align_bytes=64)
         hs = keep.tile([P, S], U8, name="hs", align_bytes=64)
@@ -58,32 +60,29 @@ def tile_moe_cpy_glu_gelu_kernel(
                     in_=src[:, 4 * q : 4 * q + 4, :].bitcast(I32).rearrange("e r n -> r e n"),
                 )
 
-        def load_words(tile, src, e0, e1):
-            nc.sync.dma_start(out=tile[:, e0:e1, :], in_=src[e0:e1, 0].rearrange("e p n d -> p e (n d)").bitcast(I32))
+        def load_words(eng, tile, src, e0, e1):
+            eng.dma_start(out=tile[:, e0:e1, :], in_=src[e0:e1, 0].rearrange("e p n d -> p e (n d)").bitcast(I32))
 
-        nc.vector.memset(w13s[:, : E * H // 8], 0)
-        nc.gpsimd.memset(w13s[:, E * H // 8 :], 0)
+        nc.vector.memset(xs[:], 0)
+        nc.vector.memset(w1s[:], 0)
+        nc.gpsimd.memset(w3s[:], 0)
         nc.vector.memset(zeros[:], 0.0)
         nc.vector.memset(w2s[:], 0)
         make_identity(nc, ident[:])
 
-        nc.sync.dma_start(offs_t[:], offs)
-        for q, eng in enumerate((nc.scalar, nc.scalar, nc.sync, nc.sync)):
-            eng.dma_start(
-                out=xs[32 * q : 32 * q + 32, :],
-                in_=x_scales[:, 4 * q : 4 * q + 4, :].bitcast(I32).broadcast_to([8, 4, T // 4]),
-            )
         nc.sync.dma_start(out=xw[:], in_=x_words[0].rearrange("p t d -> p (t d)").bitcast(I32))
-        load_scales(nc.sync, w13s, W1_ROW, w1_scales[:, 0])
-        load_scales(nc.scalar, w13s, W3_ROW, w3_scales[:, 0])
-        for e0, e1 in ((0, 1), (1, 3)):
-            load_words(w1, w1_words, e0, e1)
-            load_words(w3, w3_words, e0, e1)
+        for q, eng in enumerate((nc.scalar, nc.scalar, nc.sync, nc.sync)):
+            eng.dma_start(out=xs[32 * q : 32 * q + 4, :], in_=x_scales[0, 4 * q : 4 * q + 4, :].bitcast(I32))
+        nc.sync.dma_start(offs_t[:], offs)
+        load_scales(nc.scalar, w1s, W1_ROW, w1_scales[:, 0])
+        for e in range(E):
+            load_words(nc.sync, w1, w1_words, e, e + 1)
+            if e == 0:
+                load_scales(nc.sync, w3s, W3_ROW, w3_scales[:, 0])
+            load_words(nc.sync, w3, w3_words, e, e + 1)
         load_scales(nc.sync, w2s, W2_ROW, w2_scales[:, 0])
-        load_words(w1, w1_words, 3, E)
-        load_words(w3, w3_words, 3, E)
-        load_words(w2, w2_words, 0, 3)
-        load_words(w2, w2_words, 3, E)
+        for e in range(0, E, 2):
+            load_words(nc.sync, w2, w2_words, e, e + 2)
         nc.sync.dma_start(out=y[0][:, S : S + T], in_=xr[0:P, :])
         nc.sync.dma_start(out=g_t[:], in_=gate.rearrange("r p t -> p r t"))
         for r, pos in enumerate((pos1, pos2, pos3)):
@@ -102,31 +101,29 @@ def tile_moe_cpy_glu_gelu_kernel(
             nc.vector.tensor_copy(xgs[:], xs[:].bitcast(U8).indirect(lst))
             return xgw, xgs
 
-        def first_layer(j, xgw, xgs):
+        def first_layer(j, tag, bufs, words, plane, row):
             e = j // 2
+            xgw, xgs = tokens[e]
             cols = slice(j % 2 * P, (j % 2 + 1) * P)
-            scols = slice(e * H // 4, (e + 1) * H // 4)
-            a = psum.tile([P, H], F32, name="a", tag="a", bufs=2)
-            b = psum.tile([P, H], F32, name="b", tag="b", bufs=3)
-            for acc, wt, ws, row in ((a, w1, w13s, W1_ROW), (b, w3, w13s, W3_ROW)):
-                nc.tensor.matmul_mx(
-                    out=acc[:], lhsT=xgw[:, cols].bitcast(FP8X4), lhsT_scale=xgs[:, cols],
-                    rhs=wt[:, e, :].bitcast(FP8X4), rhs_scale=ws[row:P, scols].bitcast(U8), start=True, stop=True,
-                )
-            act = ring.tile([P, H], F32, name="act", align_bytes=64, bufs=6)
-            nc.scalar.activation(
-                act[:].rearrange("s (u p v) -> s u p v", u=2, v=2), a[:].rearrange("s (p u v) -> s u p v", u=2, v=2), GELU
+            acc = psum.tile([P, H], F32, name="acc", tag=tag, bufs=bufs)
+            nc.tensor.matmul_mx(
+                out=acc[:], lhsT=xgw[:, cols].bitcast(FP8X4), lhsT_scale=xgs[:, cols],
+                rhs=words[:, e, :].bitcast(FP8X4), rhs_scale=plane[row:P, e * H // 4 : (e + 1) * H // 4].bitcast(U8),
+                start=True, stop=True,
             )
+            return acc[:].rearrange("s (p u v) -> s u p v", u=2, v=2)
+
+        def activate(a):
+            act = ring.tile([P, 2, P, 2], F32, name="act", align_bytes=64, bufs=6)
+            nc.scalar.activation(act[:], a, GELU)
+            return act
+
+        def multiply(act, b):
             h = ring.tile([P, H], BF16, name="h", align_bytes=64, bufs=12)
-            nc.vector.tensor_tensor(
-                h[:].rearrange("s (u p v) -> s u p v", u=2, v=2),
-                act[:].rearrange("s (u p v) -> s u p v", u=2, v=2),
-                b[:].rearrange("s (p u v) -> s u p v", u=2, v=2),
-                MULT,
-            )
+            nc.vector.tensor_tensor(h[:].rearrange("s (u p v) -> s u p v", u=2, v=2), act[:], b, MULT)
             return h
 
-        def quantise(j0, tiles):
+        def turn(tiles):
             n = len(tiles)
             tb = psum.tile([P, n, 2, P], F32, name="tb", tag="t", bufs=3)
             for i, h in enumerate(tiles):
@@ -134,6 +131,9 @@ def tile_moe_cpy_glu_gelu_kernel(
                     nc.tensor.transpose(tb[:, i, u, :], h[:, u * 256 : (u + 1) * 256].bitcast(F32), ident[:])
             ht = pair.tile([P, n * P * 4], BF16, name="ht", align_bytes=64, bufs=7)
             nc.scalar.copy(ht[:].bitcast(F32).rearrange("p (i s u) -> p i s u", i=n, u=2), tb[:].rearrange("p i u s -> p i s u"))
+            return ht
+
+        def quantise(j0, n, ht):
             cols = slice(j0 * P, (j0 + n) * P)
             nc.vector.quantize_mx(out=hq[:, cols].bitcast(FP8X4), scales=hs[:, cols], in_=ht[:])
 
@@ -155,24 +155,35 @@ def tile_moe_cpy_glu_gelu_kernel(
             else:
                 nc.scalar.copy(y[b][:, c0 : c0 + total], yb[:])
 
-        tokens = [gather_tokens(e) for e in range(4)]
-        hidden = []
-        for j in range(2 * E):
-            hidden.append(first_layer(j, *tokens[j // 2]))
-            if j % 2 == 1 and j >= 3 and len(tokens) < E:
-                tokens.append(gather_tokens(len(tokens)))
-            if j % 2 == 1 and j >= 5:
-                quantise(j - 5, hidden[j - 5 : j - 3])
-        quantise(8, hidden[8:10])
-        quantise(10, hidden[10:11])
-        quantise(11, hidden[11:12])
+        tiles = 2 * E
+        first_of = {j: j - 1 for j in range(1, tiles - 2, 2)}
+        first_of[tiles - 2] = tiles - 2
+        first_of[tiles - 1] = tiles - 1
+        tokens, acts, ups, hidden, turned = [], [], [], [], {}
+        for step in range(-GATHER_LEAD, tiles + QUANT_LAG):
+            j = step + GATHER_LEAD
+            if j % 2 == 0 and j < tiles:
+                tokens.append(gather_tokens(j // 2))
+            if 0 <= step < tiles:
+                acts.append(activate(first_layer(step, "a", 2, w1, w1s, W1_ROW)))
+            j = step - QUANT_LAG
+            if j in first_of:
+                quantise(first_of[j], j + 1 - first_of[j], turned[j])
+            j = step - TURN_LAG
+            if j in first_of:
+                turned[j] = turn(hidden[first_of[j] : j + 1])
+            j = step - MULT_LAG
+            if 0 <= j < tiles:
+                hidden.append(multiply(acts[j], ups[j]))
+            if 0 <= step < tiles:
+                ups.append(first_layer(step, "b", 3, w3, w3s, W3_ROW))
         second_layer(0, 0, [C, C], "a", 2)
-        second_layer(0, 2 * C, [C, C], "b", 3)
-        second_layer(0, 4 * C, [C, P], "a", 2, True)
-        second_layer(0, S - P, [P], "b", 3)
+        second_layer(0, 2 * C, [C, C], "t", 3)
+        second_layer(0, 4 * C, [C, P], "t", 3, True)
+        second_layer(0, S - P, [P], "t", 3)
 
         def product(b, r, t0, t1):
-            pr = pair.tile([P, t1 - t0], F32, name="prod%d" % r, align_bytes=64, bufs=3)
+            pr = pair.tile([P, t1 - t0], F32, name="prod%d" % r, align_bytes=64, bufs=6)
             nc.vector.tensor_tensor(pr[:], y[b][:].indirect(pos_t[r][:, t0 // 16 : t1 // 16]), g_t[:, r, t0:t1], MULT)
             return pr
 

@@ -22,7 +22,8 @@ GELU = mybir.ActivationFunctionType.Gelu_apprx_tanh
 P = 128
 W1_ROW, W3_ROW, W2_ROW = 4, 8, 12
 NB = K // P
-GATHER_LEAD, MULT_LAG, TURN_LAG, QUANT_LAG = 3, 1, 4, 10
+GATHER_LEAD, MULT_LAG, TURN_LAG = 5, 1, 4
+ON_GPSIMD = (0, 2)
 
 
 def tile_moe_cpy_glu_gelu_kernel(
@@ -118,9 +119,15 @@ def tile_moe_cpy_glu_gelu_kernel(
             nc.scalar.activation(act[:], a, GELU)
             return act
 
-        def multiply(act, b):
+        def multiply(j, act, b):
             h = ring.tile([P, H], BF16, name="h", align_bytes=64, bufs=12)
-            nc.vector.tensor_tensor(h[:].rearrange("s (u p v) -> s u p v", u=2, v=2), act[:], b, MULT)
+            if j in ON_GPSIMD:
+                up = pair.tile([P, 2, P, 2], F32, name="up", align_bytes=64)
+                nc.scalar.copy(up[:], b)
+                flat = "s u p v -> s (u p v)"
+                nc.gpsimd.tensor_tensor(h[:], act[:].rearrange(flat), up[:].rearrange(flat), MULT)
+            else:
+                nc.vector.tensor_tensor(h[:].rearrange("s (u p v) -> s u p v", u=2, v=2), act[:], b, MULT)
             return h
 
         def turn(tiles):
@@ -159,82 +166,68 @@ def tile_moe_cpy_glu_gelu_kernel(
         first_of = {j: j - 1 for j in range(1, tiles - 2, 2)}
         first_of[tiles - 2] = tiles - 2
         first_of[tiles - 1] = tiles - 1
-        tokens, acts, ups, hidden, turned = [], [], [], [], {}
-        for step in range(-GATHER_LEAD, tiles + QUANT_LAG):
-            j = step + GATHER_LEAD
-            if j % 2 == 0 and j < tiles:
-                tokens.append(gather_tokens(j // 2))
+        tokens, acts, hidden, turned = [], [], [], {}
+        for step in range(-GATHER_LEAD, tiles + TURN_LAG):
             if 0 <= step < tiles:
                 acts.append(activate(first_layer(step, "a", 2, w1, w1s, W1_ROW)))
-            j = step - QUANT_LAG
-            if j in first_of:
-                quantise(first_of[j], j + 1 - first_of[j], turned[j])
             j = step - TURN_LAG
             if j in first_of:
                 turned[j] = turn(hidden[first_of[j] : j + 1])
+            j = step + GATHER_LEAD
+            if j % 2 == 0 and j < tiles:
+                tokens.append(gather_tokens(j // 2))
             j = step - MULT_LAG
             if 0 <= j < tiles:
-                hidden.append(multiply(acts[j], ups[j]))
-            if 0 <= step < tiles:
-                ups.append(first_layer(step, "b", 3, w3, w3s, W3_ROW))
+                hidden.append(multiply(j, acts[j], first_layer(j, "b", 3, w3, w3s, W3_ROW)))
+        for j in sorted(first_of):
+            quantise(first_of[j], j + 1 - first_of[j], turned[j])
         second_layer(0, 0, [C, C], "a", 2)
-        second_layer(0, 2 * C, [C, C], "t", 3)
+        second_layer(0, 2 * C, [C, C], "b", 3)
         second_layer(0, 4 * C, [C, P], "t", 3, True)
-        second_layer(0, S - P, [P], "t", 3)
+        second_layer(0, S - P, [P], "a", 2)
 
         def product(b, r, t0, t1):
-            pr = pair.tile([P, t1 - t0], F32, name="prod%d" % r, align_bytes=64, bufs=6)
+            pr = pair.tile([P, t1 - t0], F32, name="prod%d" % r, align_bytes=64, bufs=7)
             nc.vector.tensor_tensor(pr[:], y[b][:].indirect(pos_t[r][:, t0 // 16 : t1 // 16]), g_t[:, r, t0:t1], MULT)
             return pr
 
         def products(b, t0, t1):
             return [product(b, r, t0, t1) for r in range(TOP)]
 
-        def sum_on_tensor(b, prods, p0, t0, n):
-            sb = psum.tile([P, n, P], F32, name="sb", tag="a", bufs=2)
-            for i in range(n):
-                c = t0 - p0 + i * P
-                for r in range(TOP):
-                    nc.tensor.matmul(
-                        sb[:, i, :], lhsT=prods[r][:, c : c + P], rhs=ident[:], start=(r == 0), stop=(r == TOP - 1), is_transpose=True
-                    )
-            st = pair.tile([P, n, P], F32, name="st", align_bytes=64)
-            nc.scalar.copy(st[:], sb[:])
-            bb = psum.tile([P, n, P], F32, name="bb", tag="b", bufs=3)
-            for i in range(n):
-                nc.tensor.transpose(bb[:, i, :], st[:, i, :], ident[:])
-            o = ring.tile([P, n * P], F32, name="o", align_bytes=64)
-            nc.scalar.copy(o[:], bb[:].rearrange("p i t -> p (i t)"))
-            nc.sync.dma_start(out=out[b * P : (b + 1) * P, t0 : t0 + n * P], in_=o[:])
-
         half = T // 2
+        chunks = half // P
+
+        def sum_on_tensor(b, prods, p0, t0):
+            banks = [psum.tile([P, P], F32, name="sb", tag="t", bufs=3) for i in range(chunks)]
+            for r in range(TOP):
+                for i in range(chunks):
+                    c = t0 - p0 + i * P
+                    nc.tensor.matmul(
+                        banks[i][:], lhsT=prods[r][:, c : c + P], rhs=ident[:], start=(r == 0), stop=(r == TOP - 1), is_transpose=True
+                    )
+            st = pair.tile([P, chunks, P], F32, name="st", align_bytes=64)
+            bb = psum.tile([P, chunks, P], F32, name="bb", tag="b", bufs=3)
+            for i in range(chunks):
+                nc.scalar.copy(st[:, i, :], banks[i][:])
+                nc.tensor.transpose(bb[:, i, :], st[:, i, :], ident[:])
+            o = ring.tile([P, half], F32, name="o", align_bytes=64)
+            nc.scalar.copy(o[:], bb[:].rearrange("p i t -> p (i t)"))
+            nc.sync.dma_start(out=out[b * P : (b + 1) * P, t0 : t0 + half], in_=o[:])
+
         prods = products(0, 0, T)
         for b in range(1, NB):
             for e in range(0, E, 2):
                 second_layer(b, e * C, [C, C], "t", 3)
-        for b in range(NB - 1):
-            sum_on_tensor(b, prods, 0, 0, 3)
-            sum_on_tensor(b, prods, 0, half, 3)
-            if b + 1 < NB - 1:
-                prods = products(b + 1, 0, T)
+        sum_on_tensor(0, prods, 0, 0)
+        sum_on_tensor(0, prods, 0, half)
+        prods = products(1, 0, T)
+        sum_on_tensor(1, prods, 0, 0)
+        sum_on_tensor(1, prods, 0, half)
+        for b, t0 in ((2, 0), (2, half), (3, 0)):
+            sum_on_tensor(b, products(b, t0, t0 + half), t0, t0)
+
         b = NB - 1
         rows = slice(b * P, (b + 1) * P)
-        prods = products(b, 0, half)
-        banks = [psum.tile([P, P], F32, name="sb", tag="t", bufs=3) for i in range(3)]
-        for r in range(TOP):
-            for i in range(3):
-                nc.tensor.matmul(
-                    banks[i][:], lhsT=prods[r][:, i * P : (i + 1) * P], rhs=ident[:], start=(r == 0), stop=(r == TOP - 1), is_transpose=True
-                )
-        st = pair.tile([P, 3, P], F32, name="st", align_bytes=64)
-        bb = psum.tile([P, 3, P], F32, name="bb", tag="b", bufs=3)
-        for i in range(3):
-            nc.scalar.copy(st[:, i, :], banks[i][:])
-            nc.tensor.transpose(bb[:, i, :], st[:, i, :], ident[:])
-        o = ring.tile([P, half], F32, name="o", align_bytes=64)
-        nc.scalar.copy(o[:], bb[:].rearrange("p i t -> p (i t)"))
-        nc.sync.dma_start(out=out[rows, 0:half], in_=o[:])
-
         cut = T - P
         p1 = product(b, 0, half, T)
         p2 = product(b, 1, half, T)

from contextlib import ExitStack

import concourse.mybir as mybir
from concourse.masks import make_identity

K, T, E, C, H, TOP, PAD = 512, 768, 6, 256, 512, 3, 64
S = E * C
W = S + T + PAD
FLOPS = 2 * S * (2 * K * H + H * K)

F32 = mybir.dt.float32
BF16 = mybir.dt.bfloat16
I32 = mybir.dt.int32
U32 = mybir.dt.uint32
U16 = mybir.dt.uint16
U8 = mybir.dt.uint8
FP8X4 = mybir.dt.float8_e4m3fn_x4
MULT = mybir.AluOpType.mult
ADD = mybir.AluOpType.add
GELU = mybir.ActivationFunctionType.Gelu_apprx_tanh

P = 128
W1_ROW, W3_ROW, W2_ROW = 4, 8, 12
NB = K // P
GATHER_LEAD, MULT_LAG, TURN_LAG = 5, 1, 4
ON_GPSIMD = (0, 2)


def tile_moe_cpy_glu_gelu_kernel(
    tc, x_words, x_scales, xr, w1_words, w1_scales, w3_words, w3_scales, w2_words, w2_scales, gate, offs, pos1, pos2, pos3, out
):
    nc = tc.nc
    with ExitStack() as ctx:
        keep = ctx.enter_context(tc.tile_pool(name="keep", bufs=1))
        ring = ctx.enter_context(tc.tile_pool(name="ring", bufs=4))
        pair = ctx.enter_context(tc.tile_pool(name="pair", bufs=2))
        trio = ctx.enter_context(tc.tile_pool(name="trio", bufs=3))
        psum = ctx.enter_context(tc.psum_pool(name="psum", bufs=2))

        offs_t = keep.tile([P, S // 16], U16, name="offs_t")
        pos_t = [keep.tile([P, T // 16], U16, name="pos%d_t" % r) for r in range(TOP)]
        xw = keep.tile([P, T], I32, name="xw", align_bytes=64)
        xs = keep.tile([P, T // 4], I32, name="xs", align_bytes=64)
        w1 = keep.tile([P, E, H], I32, name="w1", align_bytes=64)
        w3 = keep.tile([P, E, H], I32, name="w3", align_bytes=64)
        w2 = keep.tile([P, E, K], I32, name="w2", align_bytes=64)
        w1s = keep.tile([P, E * H // 4], I32, name="w1s", align_bytes=64)
        w3s = keep.tile([P, E * H // 4], I32, name="w3s", align_bytes=64)
        w2s = keep.tile([P, E * K // 4], I32, name="w2s", align_bytes=64)
        hq = keep.tile([P, S], U32, name="hq", align_bytes=64)
        hs = keep.tile([P, S], U8, name="hs", align_bytes=64)
        y = [keep.tile([P, W], F32, name="y%d" % b, align_bytes=64) for b in range(NB)]
        g_t = keep.tile([P, TOP, T], F32, name="g_t", align_bytes=64)
        ident = keep.tile([P, P], F32, name="ident", align_bytes=64)
        zeros = keep.tile([P, PAD], F32, name="zeros")

        def load_scales(eng, tile, row, src):
            for q in range(4):
                eng.dma_start(
                    out=tile[32 * q + row : 32 * q + row + 4, :].rearrange("r (e n) -> r e n", e=src.shape[0]),
                    in_=src[:, 4 * q : 4 * q + 4, :].bitcast(I32).rearrange("e r n -> r e n"),
                )

        def load_words(eng, tile, src, e0, e1):
            eng.dma_start(out=tile[:, e0:e1, :], in_=src[e0:e1, 0].rearrange("e p n d -> p e (n d)").bitcast(I32))

        nc.vector.memset(xs[:], 0)
        nc.vector.memset(w1s[:], 0)
        nc.gpsimd.memset(w3s[:], 0)
        nc.vector.memset(zeros[:], 0.0)
        nc.vector.memset(w2s[:], 0)
        make_identity(nc, ident[:])

        nc.sync.dma_start(out=xw[:], in_=x_words[0].rearrange("p t d -> p (t d)").bitcast(I32))
        for q, eng in enumerate((nc.scalar, nc.scalar, nc.sync, nc.sync)):
            eng.dma_start(out=xs[32 * q : 32 * q + 4, :], in_=x_scales[0, 4 * q : 4 * q + 4, :].bitcast(I32))
        nc.sync.dma_start(offs_t[:], offs)
        load_scales(nc.scalar, w1s, W1_ROW, w1_scales[:, 0])
        for e in range(E):
            load_words(nc.sync, w1, w1_words, e, e + 1)
            if e == 0:
                load_scales(nc.sync, w3s, W3_ROW, w3_scales[:, 0])
            load_words(nc.sync, w3, w3_words, e, e + 1)
        load_scales(nc.sync, w2s, W2_ROW, w2_scales[:, 0])
        for e in range(0, E, 2):
            load_words(nc.sync, w2, w2_words, e, e + 2)
        nc.sync.dma_start(out=y[0][:, S : S + T], in_=xr[0:P, :])
        nc.sync.dma_start(out=g_t[:], in_=gate.rearrange("r p t -> p r t"))
        for r, pos in enumerate((pos1, pos2, pos3)):
            nc.sync.dma_start(pos_t[r][:], pos)
        for b in range(1, NB):
            nc.sync.dma_start(out=y[b][:, S : S + T], in_=xr[b * P : (b + 1) * P, :])

        for b in range(NB):
            nc.scalar.activation(y[b][:, S + T : W], zeros[:], GELU)

        def gather_tokens(e):
            lst = offs_t[:, e * C // 16 : (e + 1) * C // 16]
            xgw = trio.tile([P, C], U32, name="xgw", align_bytes=64)
            xgs = trio.tile([P, C], U8, name="xgs", align_bytes=64)
            nc.vector.tensor_copy(xgw[:], xw[:].bitcast(U32).indirect(lst))
            nc.vector.tensor_copy(xgs[:], xs[:].bitcast(U8).indirect(lst))
            return xgw, xgs

        def first_layer(j, tag, bufs, words, plane, row):
            e = j // 2
            xgw, xgs = tokens[e]
            cols = slice(j % 2 * P, (j % 2 + 1) * P)
            acc = psum.tile([P, H], F32, name="acc", tag=tag, bufs=bufs)
            nc.tensor.matmul_mx(
                out=acc[:], lhsT=xgw[:, cols].bitcast(FP8X4), lhsT_scale=xgs[:, cols],
                rhs=words[:, e, :].bitcast(FP8X4), rhs_scale=plane[row:P, e * H // 4 : (e + 1) * H // 4].bitcast(U8),
                start=True, stop=True,
            )
            return acc[:].rearrange("s (p u v) -> s u p v", u=2, v=2)

        def activate(a):
            act = ring.tile([P, 2, P, 2], F32, name="act", align_bytes=64, bufs=6)
            nc.scalar.activation(act[:], a, GELU)
            return act

        def multiply(j, act, b):
            h = ring.tile([P, H], BF16, name="h", align_bytes=64, bufs=12)
            if j in ON_GPSIMD:
                up = pair.tile([P, 2, P, 2], F32, name="up", align_bytes=64)
                nc.scalar.copy(up[:], b)
                flat = "s u p v -> s (u p v)"
                nc.gpsimd.tensor_tensor(h[:], act[:].rearrange(flat), up[:].rearrange(flat), MULT)
            else:
                nc.vector.tensor_tensor(h[:].rearrange("s (u p v) -> s u p v", u=2, v=2), act[:], b, MULT)
            return h

        def turn(tiles):
            n = len(tiles)
            tb = psum.tile([P, n, 2, P], F32, name="tb", tag="t", bufs=3)
            for i, h in enumerate(tiles):
                for u in range(2):
                    nc.tensor.transpose(tb[:, i, u, :], h[:, u * 256 : (u + 1) * 256].bitcast(F32), ident[:])
            ht = pair.tile([P, n * P * 4], BF16, name="ht", align_bytes=64, bufs=7)
            nc.scalar.copy(ht[:].bitcast(F32).rearrange("p (i s u) -> p i s u", i=n, u=2), tb[:].rearrange("p i u s -> p i s u"))
            return ht

        def quantise(j0, n, ht):
            cols = slice(j0 * P, (j0 + n) * P)
            nc.vector.quantize_mx(out=hq[:, cols].bitcast(FP8X4), scales=hs[:, cols], in_=ht[:])

        def second_layer(b, c0, widths, tag, bufs, on_vector=False):
            total = sum(widths)
            yb = psum.tile([P, total], F32, name="yb", tag=tag, bufs=bufs)
            c = c0
            for wd in widths:
                e = c // C
                sc = e * K // 4 + b * P // 4
                nc.tensor.matmul_mx(
                    out=yb[:, c - c0 : c - c0 + wd], lhsT=w2[:, e, b * P : (b + 1) * P].bitcast(FP8X4),
                    lhsT_scale=w2s[W2_ROW:P, sc : sc + P // 4].bitcast(U8),
                    rhs=hq[:, c : c + wd].bitcast(FP8X4), rhs_scale=hs[:, c : c + wd], start=True, stop=True,
                )
                c += wd
            if on_vector:
                nc.vector.tensor_copy(y[b][:, c0 : c0 + total], yb[:])
            else:
                nc.scalar.copy(y[b][:, c0 : c0 + total], yb[:])

        tiles = 2 * E
        first_of = {j: j - 1 for j in range(1, tiles - 2, 2)}
        first_of[tiles - 2] = tiles - 2
        first_of[tiles - 1] = tiles - 1
        tokens, acts, hidden, turned = [], [], [], {}
        for step in range(-GATHER_LEAD, tiles + TURN_LAG):
            if 0 <= step < tiles:
                acts.append(activate(first_layer(step, "a", 2, w1, w1s, W1_ROW)))
            j = step - TURN_LAG
            if j in first_of:
                turned[j] = turn(hidden[first_of[j] : j + 1])
            j = step + GATHER_LEAD
            if j % 2 == 0 and j < tiles:
                tokens.append(gather_tokens(j // 2))
            j = step - MULT_LAG
            if 0 <= j < tiles:
                hidden.append(multiply(j, acts[j], first_layer(j, "b", 3, w3, w3s, W3_ROW)))
        for j in sorted(first_of):
            quantise(first_of[j], j + 1 - first_of[j], turned[j])
        second_layer(0, 0, [C, C], "a", 2)
        second_layer(0, 2 * C, [C, C], "b", 3)
        second_layer(0, 4 * C, [C, P], "t", 3, True)
        second_layer(0, S - P, [P], "a", 2)

        def product(b, r, t0, t1):
            pr = pair.tile([P, t1 - t0], F32, name="prod%d" % r, align_bytes=64, bufs=7)
            nc.vector.tensor_tensor(pr[:], y[b][:].indirect(pos_t[r][:, t0 // 16 : t1 // 16]), g_t[:, r, t0:t1], MULT)
            return pr

        def products(b, t0, t1):
            return [product(b, r, t0, t1) for r in range(TOP)]

        half = T // 2
        chunks = half // P

        def sum_on_tensor(b, prods, p0, t0):
            banks = [psum.tile([P, P], F32, name="sb", tag="t", bufs=3) for i in range(chunks)]
            for r in range(TOP):
                for i in range(chunks):
                    c = t0 - p0 + i * P
                    nc.tensor.matmul(
                        banks[i][:], lhsT=prods[r][:, c : c + P], rhs=ident[:], start=(r == 0), stop=(r == TOP - 1), is_transpose=True
                    )
            st = pair.tile([P, chunks, P], F32, name="st", align_bytes=64)
            bb = psum.tile([P, chunks, P], F32, name="bb", tag="b", bufs=3)
            for i in range(chunks):
                nc.scalar.copy(st[:, i, :], banks[i][:])
                nc.tensor.transpose(bb[:, i, :], st[:, i, :], ident[:])
            o = ring.tile([P, half], F32, name="o", align_bytes=64)
            nc.scalar.copy(o[:], bb[:].rearrange("p i t -> p (i t)"))
            nc.sync.dma_start(out=out[b * P : (b + 1) * P, t0 : t0 + half], in_=o[:])

        prods = products(0, 0, T)
        for b in range(1, NB):
            for e in range(0, E, 2):
                second_layer(b, e * C, [C, C], "t", 3)
        sum_on_tensor(0, prods, 0, 0)
        sum_on_tensor(0, prods, 0, half)
        prods = products(1, 0, T)
        sum_on_tensor(1, prods, 0, 0)
        sum_on_tensor(1, prods, 0, half)
        for b, t0 in ((2, 0), (2, half), (3, 0)):
            sum_on_tensor(b, products(b, t0, t0 + half), t0, t0)

        b = NB - 1
        rows = slice(b * P, (b + 1) * P)
        cut = T - P
        p1 = product(b, 0, half, T)
        p2 = product(b, 1, half, T)
        p3a = product(b, 2, half, cut)
        s12 = pair.tile([P, half], F32, name="s12", align_bytes=64)
        nc.vector.tensor_tensor(s12[:], p1[:], p2[:], ADD)
        p3b = product(b, 2, cut, T)
        for p3, t0, t1 in ((p3a, half, cut), (p3b, cut, T)):
            o = ring.tile([P, t1 - t0], F32, name="o", align_bytes=64)
            nc.vector.tensor_tensor(o[:], s12[:, t0 - half : t1 - half], p3[:], ADD)
            nc.sync.dma_start(out=out[rows, t0:t1], in_=o[:])
